import numpy as np
import ml_dtypes


def mxq(x, axis, fmt="e4m3"):
    dtype, down = {"e4m3": (ml_dtypes.float8_e4m3fn, 7), "e5m2": (ml_dtypes.float8_e5m2, 14)}[fmt]
    v = np.moveaxis(np.asarray(x, np.float32).astype(ml_dtypes.bfloat16).astype(np.float64), axis, -1)
    blocks = v.reshape(v.shape[:-1] + (-1, 32))
    amax = np.abs(blocks).max(-1, keepdims=True)
    byte = np.maximum(np.where(amax > 0, np.frexp(amax)[1] - 1 + 127, 0) - down, 1)
    scale = np.exp2(byte - 127.0)
    codes = (blocks / scale).astype(np.float32).astype(dtype).astype(np.float64)
    return np.moveaxis((codes * scale).reshape(v.shape), -1, axis)


WIDE = False


def mx_kscale(k):
    if not WIDE:
        return np.ones(k)
    levels = np.array([30, -30])
    if k % 512:
        return np.exp2(np.random.permutation(np.resize(levels, k // 32))).repeat(32)
    a = np.empty((k // 512, 16))
    for p in range(k // 512):
        a[p, :8] = np.random.permutation(np.resize(levels, 8))
        for g in range(8):
            far = levels[np.abs(levels - a[p, g]) >= 10]
            a[p, g + 8] = far[np.random.randint(len(far))]
    return np.exp2(a.ravel()).repeat(32)


def f64(x):
    return np.asarray(x).astype(np.float64)


def striped(idx):
    return np.tile(np.asarray(idx).reshape(-1, 16).T, (8, 1)).astype(np.uint16)


def unstriped(offs):
    return offs[:16].T.reshape(-1).astype(np.int64)


E2M1 = np.array([0.0, 0.5, 1.0, 1.5, 2.0, 3.0, 4.0, 6.0, -0.0, -0.5, -1.0, -1.5, -2.0, -3.0, -4.0, -6.0])


def pack_weight(w, fmt):
    k, n = w.shape
    w = f64(np.asarray(w, np.float32).astype(ml_dtypes.bfloat16)).reshape(k // 32, 32, n)
    amax = np.abs(w).max(1)
    if fmt in ("e4m3", "e5m2"):
        byte = np.frexp(amax)[1] - 1 + 127 - (7 if fmt == "e4m3" else 14)
    else:
        mant, ex = np.frexp(amax / 6.0)
        byte = np.where(mant > 0.5, ex, ex - 1) + 127
    byte = np.clip(np.where(amax > 0, byte, 1), 1, 254)
    scaled = (w * np.exp2(127.0 - byte)[:, None, :]).reshape(k, n).astype(np.float32)
    by_word = np.ascontiguousarray(scaled.reshape(k // 512, 128, 4, n).transpose(0, 1, 3, 2))
    if fmt in ("e4m3", "e5m2"):
        words = by_word.astype(ml_dtypes.float8_e4m3fn if fmt == "e4m3" else ml_dtypes.float8_e5m2).view(np.uint8)
    else:
        c = by_word.astype(ml_dtypes.float4_e2m1fn).view(np.uint8) & 0xF
        words = (c[..., 0::2] | (c[..., 1::2] << 4)).reshape(k // 512, 128, 2 * n)
    return np.ascontiguousarray(words), np.ascontiguousarray(byte.astype(np.uint8).reshape(k // 512, 16, n))


def unpack_weight(words, scales, fmt):
    g, _, n = scales.shape
    words = np.ascontiguousarray(words).reshape(g, 128, n, -1)
    if fmt in ("e4m3", "e5m2"):
        vals = words.view(ml_dtypes.float8_e4m3fn if fmt == "e4m3" else ml_dtypes.float8_e5m2).astype(np.float64)
    else:
        nib = np.empty((g, 128, n, 4), np.uint8)
        nib[..., 0::2] = words & 0xF
        nib[..., 1::2] = words >> 4
        vals = E2M1[nib]
    vals = vals * np.repeat(np.exp2(scales.astype(np.float64) - 127.0), 8, axis=1)[..., None]
    return vals.transpose(0, 1, 3, 2).reshape(g * 512, n)


K, T, Z, J, R, C, N, E = 512, 1024, 1024, 256, 512, 512, 256, 128


def setup_inputs():
    n = np.random.standard_normal
    idx = np.random.permutation(T)[:J]
    idx2 = np.random.permutation(Z)[:J]
    idx3 = np.random.permutation(C)[:J]
    idx4 = np.random.permutation(C)[:J]
    idx5 = np.random.permutation(J)[:E]
    idx6 = np.random.permutation(J)[:E]
    fk = mx_kscale(K)
    fr = mx_kscale(R)
    xtp = pack_weight(n((K, T)) / fk[:, None], "e5m2")
    xop = pack_weight(n((K, Z)) / fk[:, None], "e4m3")
    wp = pack_weight(n((K, R)) * 1 / np.sqrt(K) * fk[:, None] * fr, "e2m1")
    wbp = pack_weight(n((R, N)) * 1 / np.sqrt(R) / fr[:, None], "e2m1")
    return {
        "xt_words": xtp[0],
        "xt_scales": xtp[1],
        "xo_words": xop[0],
        "xo_scales": xop[1],
        "w_words": wp[0],
        "w_scales": wp[1],
        "wb_words": wbp[0],
        "wb_scales": wbp[1],
        "offs": striped(idx),
        "offs2": striped(idx2),
        "offs3": striped(idx3),
        "offs4": striped(idx4),
        "offs5": striped(idx5),
        "offs6": striped(idx6),
    }


def reference(xt_words, xt_scales, xo_words, xo_scales, w_words, w_scales, wb_words, wb_scales, offs, offs2, offs3, offs4, offs5, offs6):
    idx = unstriped(offs)
    idx2 = unstriped(offs2)
    idx3 = unstriped(offs3)
    idx4 = unstriped(offs4)
    idx5 = unstriped(offs5)
    idx6 = unstriped(offs6)
    xtu = unpack_weight(xt_words, xt_scales, "e5m2")
    xou = unpack_weight(xo_words, xo_scales, "e4m3")
    wu = unpack_weight(w_words, w_scales, "e2m1")
    wbu = unpack_weight(wb_words, wb_scales, "e2m1")
    xtidxg = xtu[:, idx]
    a = wu.T @ xtidxg
    xoidx2g = xou[:, idx2]
    b = wu.T @ xoidx2g
    pw = np.zeros((R, C))
    pw[:, idx3] = a
    hid = np.abs(pw[:, idx4] - b)
    hidq = mxq(hid, 0, "e4m3")
    p = wbu.T @ hidq
    y = np.maximum(p[:, idx5], p[:, idx6])
    return y

@@ -1,0 +1,200 @@
+from contextlib import ExitStack
+
+import concourse.mybir as mybir
+
+K, T, Z, J, R, C, N, E = 512, 1024, 1024, 256, 512, 512, 256, 128
+FLOPS = 2 * K * R * J * 2 + 2 * R * N * J
+
+F32 = mybir.dt.float32
+BF16 = mybir.dt.bfloat16
+I32 = mybir.dt.int32
+U32 = mybir.dt.uint32
+U16 = mybir.dt.uint16
+U8 = mybir.dt.uint8
+E4M3 = mybir.dt.float8_e4m3fn_x4
+E5M2 = mybir.dt.float8_e5m2_x4
+E2M1 = mybir.dt.float4_e2m1fn_x4
+ACT = mybir.ActivationFunctionType
+ALU = mybir.AluOpType
+
+P = 128
+PACK = 4
+HALF = J // 2
+
+
+def tile_list_oneforboth_board_one_bestoftwo_kernel(
+    tc, xt_words, xt_scales, xo_words, xo_scales, w_words, w_scales, wb_words, wb_scales,
+    offs, offs2, offs3, offs4, offs5, offs6, out,
+):
+    nc = tc.nc
+    with ExitStack() as ctx:
+        lists = ctx.enter_context(tc.tile_pool(name="lists", bufs=1))
+        sb = ctx.enter_context(tc.tile_pool(name="sb", bufs=1))
+        psum = ctx.enter_context(tc.psum_pool(name="psum", bufs=1))
+
+        def load_list(name, src):
+            tile = lists.tile(list(src.shape), U16, name=name)
+            nc.sync.dma_start(tile[:], src)
+            return tile
+
+        def load_plane(name, src, queue):
+            width = src.shape[2] // 4
+            tile = sb.tile([P, src.shape[2]], U8, name=name, align_bytes=64)
+            for q in range(4):
+                rows = src[0, 4 * q : 4 * q + 4, :].bitcast(I32)
+                queue.dma_start(tile[32 * q : 32 * q + 32, :].bitcast(I32), rows.unsqueeze(0).to_broadcast([8, 4, width]))
+            return tile
+
+        def load_words(name, src, queue=nc.sync):
+            tile = sb.tile([P, src.shape[1] // 4], I32, name=name, align_bytes=64)
+            queue.dma_start(tile[:], src.bitcast(I32))
+            return tile
+
+        boards = []
+        for t in range(PACK):
+            board = sb.tile([P, C], F32, name="board%d" % t)
+            nc.vector.memset(board[:], 0.0)
+            boards.append(board)
+
+        l1 = load_list("l1", offs)
+        xt_plane = load_plane("xt_plane", xt_scales, nc.scalar)
+        w_raw = load_words("w_raw", w_words[0])
+        xt_table = load_words("xt_table", xt_words[0].rearrange("p n t -> p (n t)"))
+        w_plane = load_plane("w_plane", w_scales, nc.sync)
+        l3 = load_list("l3", offs3)
+        xo_table = load_words("xo_table", xo_words[0].rearrange("p n t -> p (n t)"))
+        l2 = load_list("l2", offs2)
+        xo_plane = load_plane("xo_plane", xo_scales, nc.sync)
+        l4 = load_list("l4", offs4)
+        wb_raw = load_words("wb_raw", wb_words[0])
+        wb_plane = load_plane("wb_plane", wb_scales, nc.sync)
+        l5 = load_list("l5", offs5)
+        l6 = load_list("l6", offs6)
+
+        xt_s = sb.tile([P, J], U8, name="xt_s", align_bytes=64)
+        nc.vector.tensor_copy(xt_s[:], xt_plane[:].indirect(l1[:]))
+        w_dealt = sb.tile([P, 2 * R], U8, name="w_dealt", align_bytes=64)
+        nc.scalar.copy(
+            w_dealt[:].bitcast(U16).rearrange("p (t m) -> p t m", t=PACK),
+            w_raw[:].bitcast(U16).rearrange("p (m t) -> p t m", t=PACK),
+        )
+        xt_c = sb.tile([P, J], U32, name="xt_c", align_bytes=64)
+        nc.vector.tensor_copy(xt_c[:], xt_table[:].bitcast(U32).indirect(l1[:]))
+        ws_dealt = sb.tile([P, R], U8, name="ws_dealt", align_bytes=64)
+        for lo, hi in ((0, 2), (2, PACK)):
+            nc.vector.tensor_copy(
+                ws_dealt[:].rearrange("p (t m) -> p t m", t=PACK)[:, lo:hi, :],
+                w_plane[:].rearrange("p (m t) -> p t m", t=PACK)[:, lo:hi, :],
+            )
+
+        def first_product(dst, t, codes, scales, fmt):
+            nc.tensor.matmul_mx(
+                out=dst,
+                lhsT=w_dealt[:, 2 * P * t : 2 * P * (t + 1)].bitcast(E2M1),
+                lhsT_scale=ws_dealt[:, P * t : P * (t + 1)],
+                rhs=codes.bitcast(fmt),
+                rhs_scale=scales,
+                start=True,
+                stop=True,
+            )
+
+        a_ps = []
+        for t in range(PACK):
+            bank = psum.tile([P, J], F32, name="a_ps%d" % t, tag="bank%d" % t)
+            first_product(bank[:], t, xt_c[:], xt_s[:], E5M2)
+            a_ps.append(bank)
+
+        a_sb = [sb.tile([P, J], F32, name="a_sb%d" % t) for t in range(PACK)]
+        picked = sb.tile([P, PACK, J], F32, name="picked")
+
+        def fetch(t):
+            nc.scalar.activation(a_sb[t][:], a_ps[t][:], ACT.Copy)
+
+        def put(on_scalar, t):
+            if on_scalar:
+                nc.scalar.activation(boards[t][:].indirect(l3[:]), a_sb[t][:], ACT.Copy)
+            else:
+                nc.vector.tensor_copy(boards[t][:].indirect(l3[:]), a_sb[t][:])
+
+        def pick(on_scalar, dst, window, offsets):
+            if on_scalar:
+                nc.scalar.activation(dst, window.indirect(offsets), ACT.Copy)
+            else:
+                nc.vector.tensor_copy(dst, window.indirect(offsets))
+
+        def pick_half(on_scalar, t, h):
+            pick(on_scalar, picked[:, t, h * HALF : (h + 1) * HALF], boards[t][:], l4[:, 8 * h : 8 * h + 8])
+
+        fetch(0)
+        fetch(1)
+        put(False, 0)
+        put(True, 1)
+        fetch(2)
+        fetch(3)
+
+        xo_s = sb.tile([P, J], U8, name="xo_s", align_bytes=64)
+        nc.vector.tensor_copy(xo_s[:], xo_plane[:].indirect(l2[:]))
+        xo_c = sb.tile([P, J], U32, name="xo_c", align_bytes=64)
+        nc.vector.tensor_copy(xo_c[:], xo_table[:].bitcast(U32).indirect(l2[:]))
+        b_ps = []
+        for h in range(2):
+            bank = psum.tile([P, PACK, HALF], F32, name="b_ps%d" % h, tag="bank%d" % (4 + h))
+            cols = slice(h * HALF, (h + 1) * HALF)
+            for t in range(PACK):
+                first_product(bank[:, t, :], t, xo_c[:, cols], xo_s[:, cols], E4M3)
+            b_ps.append(bank)
+
+        put(False, 2)
+        put(True, 3)
+
+        diffs = [sb.tile([P, PACK, HALF], F32, name="diff%d" % h) for h in range(2)]
+
+        def subtract(h):
+            nc.vector.tensor_tensor(diffs[h][:], picked[:, :, h * HALF : (h + 1) * HALF], b_ps[h][:], ALU.subtract)
+
+        pick_half(True, 1, 0)
+        pick_half(True, 3, 0)
+        pick_half(True, 0, 0)
+        pick(False, picked[:, 2, :], boards[2][:], l4[:])
+        subtract(0)
+        pick_half(True, 1, 1)
+        pick_half(True, 3, 1)
+        pick_half(False, 0, 1)
+        subtract(1)
+
+        p_sb = [sb.tile([P, J], F32, name="p_sb%d" % u) for u in range(2)]
+        for h in range(2):
+            cols = slice(h * HALF, (h + 1) * HALF)
+            hid = sb.tile([P, HALF * PACK], BF16, name="hid%d" % h, align_bytes=64)
+            nc.scalar.activation(
+                hid[:].rearrange("p (c i t) -> p c t i", i=4, t=PACK),
+                diffs[h][:].rearrange("p t (c i) -> p c t i", i=4),
+                ACT.Abs,
+            )
+            hid_c = sb.tile([P, HALF], U32, name="hid_c%d" % h, align_bytes=64)
+            hid_s = sb.tile([P, HALF], U8, name="hid_s%d" % h, align_bytes=64)
+            nc.vector.quantize_mx(out=hid_c[:].bitcast(E4M3), scales=hid_s[:], in_=hid[:])
+            for u in range(2):
+                bank = psum.tile([P, HALF], F32, name="p_ps%d%d" % (h, u), tag="bank%d" % (2 * h + u))
+                nc.tensor.matmul_mx(
+                    out=bank[:],
+                    lhsT=wb_raw[:].bitcast(U8)[:, 2 * P * u : 2 * P * (u + 1)].bitcast(E2M1),
+                    lhsT_scale=wb_plane[:, P * u : P * (u + 1)],
+                    rhs=hid_c[:].bitcast(E4M3),
+                    rhs_scale=hid_s[:],
+                    start=True,
+                    stop=True,
+                )
+                if h == 1 and u == 1:
+                    nc.scalar.activation(p_sb[u][:, cols], bank[:], ACT.Copy)
+                else:
+                    nc.vector.tensor_copy(p_sb[u][:, cols], bank[:])
+
+        first = sb.tile([P, 2, E], F32, name="first")
+        second = sb.tile([P, 2, E], F32, name="second")
+        for u in range(2):
+            pick(u == 1, first[:, u, :], p_sb[u][:], l5[:])
+            pick(u == 1, second[:, u, :], p_sb[u][:], l6[:])
+        best = sb.tile([P, 2, E], F32, name="best")
+        nc.vector.tensor_tensor(best[:], first[:], second[:], ALU.max)
+        nc.sync.dma_start(out.rearrange("(u p) e -> p u e", p=P), best[:])

@@ -37,15 +37,15 @@ def tile_list_oneforboth_board_one_bestoftwo_kernel(
             nc.sync.dma_start(tile[:], src)
             return tile
 
-        def load_plane(name, src, queue):
+        def load_plane(name, src, queues):
             width = src.shape[2] // 4
-            tile = sb.tile([P, src.shape[2]], U8, name=name, align_bytes=64)
-            for q in range(4):
+            tile = sb.tile([P, src.shape[2]], U8, name=name, tag=name, align_bytes=64)
+            for q, queue in enumerate(queues):
                 rows = src[0, 4 * q : 4 * q + 4, :].bitcast(I32)
                 queue.dma_start(tile[32 * q : 32 * q + 32, :].bitcast(I32), rows.unsqueeze(0).to_broadcast([8, 4, width]))
             return tile
 
-        def load_words(name, src, queue=nc.sync):
+        def load_words(name, src, queue):
             tile = sb.tile([P, src.shape[1] // 4], I32, name=name, align_bytes=64)
             queue.dma_start(tile[:], src.bitcast(I32))
             return tile
@@ -56,18 +56,19 @@ def tile_list_oneforboth_board_one_bestoftwo_kernel(
             nc.vector.memset(board[:], 0.0)
             boards.append(board)
 
+        on_sync = [nc.sync] * 4
         l1 = load_list("l1", offs)
-        xt_plane = load_plane("xt_plane", xt_scales, nc.scalar)
-        w_raw = load_words("w_raw", w_words[0])
-        xt_table = load_words("xt_table", xt_words[0].rearrange("p n t -> p (n t)"))
-        w_plane = load_plane("w_plane", w_scales, nc.sync)
+        xt_plane = load_plane("xt_plane", xt_scales, [nc.sync, nc.scalar, nc.scalar, nc.scalar])
+        xt_table = load_words("xt_table", xt_words[0].rearrange("p n t -> p (n t)"), nc.sync)
+        w_raw = load_words("w_raw", w_words[0], nc.scalar)
+        w_plane = load_plane("w_plane", w_scales, on_sync)
         l3 = load_list("l3", offs3)
-        xo_table = load_words("xo_table", xo_words[0].rearrange("p n t -> p (n t)"))
+        xo_table = load_words("xo_table", xo_words[0].rearrange("p n t -> p (n t)"), nc.sync)
         l2 = load_list("l2", offs2)
-        xo_plane = load_plane("xo_plane", xo_scales, nc.sync)
+        xo_plane = load_plane("xo_plane", xo_scales, on_sync)
         l4 = load_list("l4", offs4)
-        wb_raw = load_words("wb_raw", wb_words[0])
-        wb_plane = load_plane("wb_plane", wb_scales, nc.sync)
+        wb_raw = load_words("wb_raw", wb_words[0], nc.sync)
+        wb_plane = load_plane("wb_plane", wb_scales, on_sync)
         l5 = load_list("l5", offs5)
         l6 = load_list("l6", offs6)
 
@@ -81,7 +82,7 @@ def tile_list_oneforboth_board_one_bestoftwo_kernel(
         xt_c = sb.tile([P, J], U32, name="xt_c", align_bytes=64)
         nc.vector.tensor_copy(xt_c[:], xt_table[:].bitcast(U32).indirect(l1[:]))
         ws_dealt = sb.tile([P, R], U8, name="ws_dealt", align_bytes=64)
-        for lo, hi in ((0, 2), (2, PACK)):
+        for lo, hi in ((0, 1), (1, PACK)):
             nc.vector.tensor_copy(
                 ws_dealt[:].rearrange("p (t m) -> p t m", t=PACK)[:, lo:hi, :],
                 w_plane[:].rearrange("p (m t) -> p t m", t=PACK)[:, lo:hi, :],
@@ -105,10 +106,12 @@ def tile_list_oneforboth_board_one_bestoftwo_kernel(
             a_ps.append(bank)
 
         a_sb = [sb.tile([P, J], F32, name="a_sb%d" % t) for t in range(PACK)]
-        picked = sb.tile([P, PACK, J], F32, name="picked")
 
         def fetch(t):
-            nc.scalar.activation(a_sb[t][:], a_ps[t][:], ACT.Copy)
+            if t == 0:
+                nc.vector.tensor_copy(a_sb[t][:], a_ps[t][:])
+            else:
+                nc.scalar.activation(a_sb[t][:], a_ps[t][:], ACT.Copy)
 
         def put(on_scalar, t):
             if on_scalar:
@@ -123,14 +126,12 @@ def tile_list_oneforboth_board_one_bestoftwo_kernel(
                 nc.vector.tensor_copy(dst, window.indirect(offsets))
 
         def pick_half(on_scalar, t, h):
-            pick(on_scalar, picked[:, t, h * HALF : (h + 1) * HALF], boards[t][:], l4[:, 8 * h : 8 * h + 8])
+            pick(on_scalar, picked[h][:, t, :], boards[t][:], l4[:, 8 * h : 8 * h + 8])
 
-        fetch(0)
-        fetch(1)
-        put(False, 0)
-        put(True, 1)
-        fetch(2)
-        fetch(3)
+        for t in range(PACK):
+            fetch(t)
+        for t in range(PACK):
+            put(t % 2 == 1, t)
 
         xo_s = sb.tile([P, J], U8, name="xo_s", align_bytes=64)
         nc.vector.tensor_copy(xo_s[:], xo_plane[:].indirect(l2[:]))
@@ -144,22 +145,24 @@ def tile_list_oneforboth_board_one_bestoftwo_kernel(
                 first_product(bank[:, t, :], t, xo_c[:, cols], xo_s[:, cols], E4M3)
             b_ps.append(bank)
 
-        put(False, 2)
-        put(True, 3)
-
+        picked = [
+            sb.tile([P, PACK, HALF], F32, name="picked%d" % h, tag=tag, align_bytes=64)
+            for h, tag in enumerate(("picked0", "xo_plane"))
+        ]
         diffs = [sb.tile([P, PACK, HALF], F32, name="diff%d" % h) for h in range(2)]
 
         def subtract(h):
-            nc.vector.tensor_tensor(diffs[h][:], picked[:, :, h * HALF : (h + 1) * HALF], b_ps[h][:], ALU.subtract)
+            nc.vector.tensor_tensor(diffs[h][:], picked[h][:], b_ps[h][:], ALU.subtract)
 
         pick_half(True, 1, 0)
-        pick_half(True, 3, 0)
         pick_half(True, 0, 0)
-        pick(False, picked[:, 2, :], boards[2][:], l4[:])
+        pick_half(True, 3, 0)
+        pick_half(False, 2, 0)
+        pick_half(False, 0, 1)
+        pick_half(False, 2, 1)
         subtract(0)
         pick_half(True, 1, 1)
         pick_half(True, 3, 1)
-        pick_half(False, 0, 1)
         subtract(1)
 
         p_sb = [sb.tile([P, J], F32, name="p_sb%d" % u) for u in range(2)]
@@ -195,6 +198,7 @@ def tile_list_oneforboth_board_one_bestoftwo_kernel(
         for u in range(2):
             pick(u == 1, first[:, u, :], p_sb[u][:], l5[:])
             pick(u == 1, second[:, u, :], p_sb[u][:], l6[:])
-        best = sb.tile([P, 2, E], F32, name="best")
-        nc.vector.tensor_tensor(best[:], first[:], second[:], ALU.max)
-        nc.sync.dma_start(out.rearrange("(u p) e -> p u e", p=P), best[:])
+        for u, queue in enumerate((nc.sync, nc.sync)):
+            best = sb.tile([P, E], F32, name="best%d" % u)
+            nc.vector.tensor_tensor(best[:], first[:, u, :], second[:, u, :], ALU.max)
+            queue.dma_start(out[P * u : P * (u + 1), :], best[:])

from contextlib import ExitStack

import concourse.mybir as mybir

K, T, Z, J, R, C, N, E = 512, 1024, 1024, 256, 512, 512, 256, 128
FLOPS = 2 * K * R * J * 2 + 2 * R * N * J

F32 = mybir.dt.float32
BF16 = mybir.dt.bfloat16
I32 = mybir.dt.int32
U32 = mybir.dt.uint32
U16 = mybir.dt.uint16
U8 = mybir.dt.uint8
E4M3 = mybir.dt.float8_e4m3fn_x4
E5M2 = mybir.dt.float8_e5m2_x4
E2M1 = mybir.dt.float4_e2m1fn_x4
ACT = mybir.ActivationFunctionType
ALU = mybir.AluOpType

P = 128
PACK = 4
HALF = J // 2


def tile_list_oneforboth_board_one_bestoftwo_kernel(
    tc, xt_words, xt_scales, xo_words, xo_scales, w_words, w_scales, wb_words, wb_scales,
    offs, offs2, offs3, offs4, offs5, offs6, out,
):
    nc = tc.nc
    with ExitStack() as ctx:
        lists = ctx.enter_context(tc.tile_pool(name="lists", bufs=1))
        sb = ctx.enter_context(tc.tile_pool(name="sb", bufs=1))
        psum = ctx.enter_context(tc.psum_pool(name="psum", bufs=1))

        def load_list(name, src):
            tile = lists.tile(list(src.shape), U16, name=name)
            nc.sync.dma_start(tile[:], src)
            return tile

        def load_plane(name, src, queues):
            width = src.shape[2] // 4
            tile = sb.tile([P, src.shape[2]], U8, name=name, tag=name, align_bytes=64)
            for q, queue in enumerate(queues):
                rows = src[0, 4 * q : 4 * q + 4, :].bitcast(I32)
                queue.dma_start(tile[32 * q : 32 * q + 32, :].bitcast(I32), rows.unsqueeze(0).to_broadcast([8, 4, width]))
            return tile

        def load_words(name, src, queue):
            tile = sb.tile([P, src.shape[1] // 4], I32, name=name, align_bytes=64)
            queue.dma_start(tile[:], src.bitcast(I32))
            return tile

        boards = []
        for t in range(PACK):
            board = sb.tile([P, C], F32, name="board%d" % t)
            nc.vector.memset(board[:], 0.0)
            boards.append(board)

        on_sync = [nc.sync] * 4
        l1 = load_list("l1", offs)
        xt_plane = load_plane("xt_plane", xt_scales, [nc.sync, nc.scalar, nc.scalar, nc.scalar])
        xt_table = load_words("xt_table", xt_words[0].rearrange("p n t -> p (n t)"), nc.sync)
        w_raw = load_words("w_raw", w_words[0], nc.scalar)
        w_plane = load_plane("w_plane", w_scales, on_sync)
        l3 = load_list("l3", offs3)
        xo_table = load_words("xo_table", xo_words[0].rearrange("p n t -> p (n t)"), nc.sync)
        l2 = load_list("l2", offs2)
        xo_plane = load_plane("xo_plane", xo_scales, on_sync)
        l4 = load_list("l4", offs4)
        wb_raw = load_words("wb_raw", wb_words[0], nc.sync)
        wb_plane = load_plane("wb_plane", wb_scales, on_sync)
        l5 = load_list("l5", offs5)
        l6 = load_list("l6", offs6)

        xt_s = sb.tile([P, J], U8, name="xt_s", align_bytes=64)
        nc.vector.tensor_copy(xt_s[:], xt_plane[:].indirect(l1[:]))
        w_dealt = sb.tile([P, 2 * R], U8, name="w_dealt", align_bytes=64)
        nc.scalar.copy(
            w_dealt[:].bitcast(U16).rearrange("p (t m) -> p t m", t=PACK),
            w_raw[:].bitcast(U16).rearrange("p (m t) -> p t m", t=PACK),
        )
        xt_c = sb.tile([P, J], U32, name="xt_c", align_bytes=64)
        nc.vector.tensor_copy(xt_c[:], xt_table[:].bitcast(U32).indirect(l1[:]))
        ws_dealt = sb.tile([P, R], U8, name="ws_dealt", align_bytes=64)
        for lo, hi in ((0, 1), (1, PACK)):
            nc.vector.tensor_copy(
                ws_dealt[:].rearrange("p (t m) -> p t m", t=PACK)[:, lo:hi, :],
                w_plane[:].rearrange("p (m t) -> p t m", t=PACK)[:, lo:hi, :],
            )

        def first_product(dst, t, codes, scales, fmt):
            nc.tensor.matmul_mx(
                out=dst,
                lhsT=w_dealt[:, 2 * P * t : 2 * P * (t + 1)].bitcast(E2M1),
                lhsT_scale=ws_dealt[:, P * t : P * (t + 1)],
                rhs=codes.bitcast(fmt),
                rhs_scale=scales,
                start=True,
                stop=True,
            )

        a_ps = []
        for t in range(PACK):
            bank = psum.tile([P, J], F32, name="a_ps%d" % t, tag="bank%d" % t)
            first_product(bank[:], t, xt_c[:], xt_s[:], E5M2)
            a_ps.append(bank)

        a_sb = [sb.tile([P, J], F32, name="a_sb%d" % t) for t in range(PACK)]

        def fetch(t):
            if t == 0:
                nc.vector.tensor_copy(a_sb[t][:], a_ps[t][:])
            else:
                nc.scalar.activation(a_sb[t][:], a_ps[t][:], ACT.Copy)

        def put(on_scalar, t):
            if on_scalar:
                nc.scalar.activation(boards[t][:].indirect(l3[:]), a_sb[t][:], ACT.Copy)
            else:
                nc.vector.tensor_copy(boards[t][:].indirect(l3[:]), a_sb[t][:])

        def pick(on_scalar, dst, window, offsets):
            if on_scalar:
                nc.scalar.activation(dst, window.indirect(offsets), ACT.Copy)
            else:
                nc.vector.tensor_copy(dst, window.indirect(offsets))

        def pick_half(on_scalar, t, h):
            pick(on_scalar, picked[h][:, t, :], boards[t][:], l4[:, 8 * h : 8 * h + 8])

        for t in range(PACK):
            fetch(t)
        for t in range(PACK):
            put(t % 2 == 1, t)

        xo_s = sb.tile([P, J], U8, name="xo_s", align_bytes=64)
        nc.vector.tensor_copy(xo_s[:], xo_plane[:].indirect(l2[:]))
        xo_c = sb.tile([P, J], U32, name="xo_c", align_bytes=64)
        nc.vector.tensor_copy(xo_c[:], xo_table[:].bitcast(U32).indirect(l2[:]))
        b_ps = []
        for h in range(2):
            bank = psum.tile([P, PACK, HALF], F32, name="b_ps%d" % h, tag="bank%d" % (4 + h))
            cols = slice(h * HALF, (h + 1) * HALF)
            for t in range(PACK):
                first_product(bank[:, t, :], t, xo_c[:, cols], xo_s[:, cols], E4M3)
            b_ps.append(bank)

        picked = [
            sb.tile([P, PACK, HALF], F32, name="picked%d" % h, tag=tag, align_bytes=64)
            for h, tag in enumerate(("picked0", "xo_plane"))
        ]
        diffs = [sb.tile([P, PACK, HALF], F32, name="diff%d" % h) for h in range(2)]

        def subtract(h):
            nc.vector.tensor_tensor(diffs[h][:], picked[h][:], b_ps[h][:], ALU.subtract)

        pick_half(True, 1, 0)
        pick_half(True, 0, 0)
        pick_half(True, 3, 0)
        pick_half(False, 2, 0)
        pick_half(False, 0, 1)
        pick_half(False, 2, 1)
        subtract(0)
        pick_half(True, 1, 1)
        pick_half(True, 3, 1)
        subtract(1)

        p_sb = [sb.tile([P, J], F32, name="p_sb%d" % u) for u in range(2)]
        for h in range(2):
            cols = slice(h * HALF, (h + 1) * HALF)
            hid = sb.tile([P, HALF * PACK], BF16, name="hid%d" % h, align_bytes=64)
            nc.scalar.activation(
                hid[:].rearrange("p (c i t) -> p c t i", i=4, t=PACK),
                diffs[h][:].rearrange("p t (c i) -> p c t i", i=4),
                ACT.Abs,
            )
            hid_c = sb.tile([P, HALF], U32, name="hid_c%d" % h, align_bytes=64)
            hid_s = sb.tile([P, HALF], U8, name="hid_s%d" % h, align_bytes=64)
            nc.vector.quantize_mx(out=hid_c[:].bitcast(E4M3), scales=hid_s[:], in_=hid[:])
            for u in range(2):
                bank = psum.tile([P, HALF], F32, name="p_ps%d%d" % (h, u), tag="bank%d" % (2 * h + u))
                nc.tensor.matmul_mx(
                    out=bank[:],
                    lhsT=wb_raw[:].bitcast(U8)[:, 2 * P * u : 2 * P * (u + 1)].bitcast(E2M1),
                    lhsT_scale=wb_plane[:, P * u : P * (u + 1)],
                    rhs=hid_c[:].bitcast(E4M3),
                    rhs_scale=hid_s[:],
                    start=True,
                    stop=True,
                )
                if h == 1 and u == 1:
                    nc.scalar.activation(p_sb[u][:, cols], bank[:], ACT.Copy)
                else:
                    nc.vector.tensor_copy(p_sb[u][:, cols], bank[:])

        first = sb.tile([P, 2, E], F32, name="first")
        second = sb.tile([P, 2, E], F32, name="second")
        for u in range(2):
            pick(u == 1, first[:, u, :], p_sb[u][:], l5[:])
            pick(u == 1, second[:, u, :], p_sb[u][:], l6[:])
        for u, queue in enumerate((nc.sync, nc.sync)):
            best = sb.tile([P, E], F32, name="best%d" % u)
            nc.vector.tensor_tensor(best[:], first[:, u, :], second[:, u, :], ALU.max)
            queue.dma_start(out[P * u : P * (u + 1), :], best[:])
